import numpy as np
import ml_dtypes


def mxq(x, axis, fmt="e4m3"):
    dtype, down = {"e4m3": (ml_dtypes.float8_e4m3fn, 7), "e5m2": (ml_dtypes.float8_e5m2, 14)}[fmt]
    v = np.moveaxis(np.asarray(x, np.float32).astype(ml_dtypes.bfloat16).astype(np.float64), axis, -1)
    blocks = v.reshape(v.shape[:-1] + (-1, 32))
    amax = np.abs(blocks).max(-1, keepdims=True)
    byte = np.maximum(np.where(amax > 0, np.frexp(amax)[1] - 1 + 127, 0) - down, 1)
    scale = np.exp2(byte - 127.0)
    codes = (blocks / scale).astype(np.float32).astype(dtype).astype(np.float64)
    return np.moveaxis((codes * scale).reshape(v.shape), -1, axis)


WIDE = False


def mx_kscale(k):
    if not WIDE:
        return np.ones(k)
    levels = np.array([10, -10, 5, -5, 0])
    if k % 512:
        return np.exp2(np.random.permutation(np.resize(levels, k // 32))).repeat(32)
    a = np.empty((k // 512, 16))
    for p in range(k // 512):
        a[p, :8] = np.random.permutation(np.resize(levels, 8))
        for g in range(8):
            far = levels[np.abs(levels - a[p, g]) >= 10]
            a[p, g + 8] = far[np.random.randint(len(far))]
    return np.exp2(a.ravel()).repeat(32)


def f64(x):
    return np.asarray(x).astype(np.float64)


def striped(idx):
    return np.tile(idx.reshape(-1, 16).T, (8, 1)).astype(np.uint16)


def unstriped(offs):
    return offs[:16].T.reshape(-1).astype(np.int64)


def gelu(v):
    return 0.5 * v * (1.0 + np.tanh(np.sqrt(2.0 / np.pi) * (v + 0.044715 * v**3)))


K, T, E, C, N = 512, 768, 9, 256, 384
TOP = 3


def by_expert(wq, xq):
    return np.concatenate([wq[e].T @ xq[:, e * C:(e + 1) * C] for e in range(E)], axis=1)


def setup_inputs():
    n = np.random.standard_normal
    s = mx_kscale(K)[:, None]
    deal = np.repeat(np.arange(E), C).reshape(TOP, T)[:, np.random.permutation(T)]
    deal = np.take_along_axis(deal, np.argsort(np.random.rand(TOP, T), axis=0), axis=0)
    for _ in range(8):
        s_, t_ = np.random.permutation(T).reshape(2, -1); r = np.random.randint(TOP, size=T // 2); x, y = deal[r, s_].copy(), deal[r, t_].copy()
        ok = ~((deal[:, s_] == y).any(0) | (deal[:, t_] == x).any(0)); deal[r[ok], s_[ok]] = y[ok]; deal[r[ok], t_[ok]] = x[ok]
    order = np.lexsort((np.random.rand(TOP * T), deal.reshape(-1)))
    slot_token = order % T; pos = np.empty(TOP * T, np.int64); pos[order] = np.arange(TOP * T); pos = pos.reshape(TOP, T)
    g = np.random.uniform(0.5, 1.5, (TOP, T)); g = g / g.sum(0)
    w_slot = np.empty(E * C)
    for r in range(TOP): w_slot[pos[r]] = g[r]
    return {
        "xT": (n((K, T)) * s).astype(np.float32),
        "w": (n((E, K, N)) / np.sqrt(K) / s[None]).astype(np.float32),
        "b": (0.3 * n((N, E))).astype(np.float32),
        "gate": np.tile(w_slot, (K, 1)).astype(np.float32),
        "offs": striped(slot_token),
        "pos1": striped(pos[0]),
        "pos2": striped(pos[1]),
        "pos3": striped(pos[2]),
    }


def reference(xT, w, b, gate, offs, pos1, pos2, pos3):
    idx = unstriped(offs)
    xq = mxq(f64(gate) * f64(xT)[:, idx], 0, "e4m3")
    y = by_expert(mxq(f64(w), 1, "e4m3"), xq)
    y = gelu(y + np.repeat(f64(b), C, axis=1))
    return y[:, unstriped(pos1)] + y[:, unstriped(pos2)] + y[:, unstriped(pos3)]

@@ -1,0 +1,191 @@
+from contextlib import ExitStack
+
+import concourse.mybir as mybir
+
+K, T, E, C, N = 512, 768, 9, 256, 384
+S = E * C
+P = 128
+PACK = 4
+NT = N // P
+PER_COL = 16
+
+FLOPS = 2 * K * N * S
+BYTES = 4 * (K * T + E * K * N + N * E + S + N * T) + 2 * P * (S + 3 * T) // PER_COL
+
+F32 = mybir.dt.float32
+BF16 = mybir.dt.bfloat16
+U32 = mybir.dt.uint32
+U16 = mybir.dt.uint16
+U8 = mybir.dt.uint8
+FP8X4 = mybir.dt.float8_e4m3fn_x4
+MULT = mybir.AluOpType.mult
+ADD = mybir.AluOpType.add
+GELU = mybir.ActivationFunctionType.Gelu_apprx_tanh
+
+SLOT_CHUNKS = [512, 512, 512, 256, 256, 128, 128]
+GATE_CHUNKS = [512, 512, 512, 768]
+LAST_SPLIT = 480
+
+
+def spans(widths):
+    starts = [sum(widths[:i]) for i in range(len(widths))]
+    return [(a, a + n) for a, n in zip(starts, widths)]
+
+
+def tile_moe_pre_lin_gelu_kernel(tc, xT, w, b, gate, offs, pos1, pos2, pos3, out):
+    nc = tc.nc
+    with ExitStack() as ctx:
+        lists = ctx.enter_context(tc.tile_pool(name="lists", bufs=1))
+        keep = ctx.enter_context(tc.tile_pool(name="keep", bufs=1))
+        ring = ctx.enter_context(tc.tile_pool(name="ring", bufs=3))
+        psum = ctx.enter_context(tc.psum_pool(name="psum", bufs=8))
+
+        offs_sb = lists.tile([P, S // PER_COL], U16, name="offs_sb")
+        pos_sb = [lists.tile([P, T // PER_COL], U16, name="pos_sb%d" % r) for r in range(3)]
+        x_rows = [keep.tile([P, T], F32, name="x_rows%d" % j) for j in range(PACK)]
+        gate_sb = keep.tile([P, S], F32, name="gate_sb")
+        w_raw = [keep.tile([P, PACK, N], F32, name="w_raw%d" % e) for e in range(E)]
+        bias = keep.tile([P, NT, 16], F32, name="bias")
+        x_bf = keep.tile([P, S, PACK], BF16, name="x_bf", align_bytes=64)
+        x_codes = keep.tile([P, S], U32, name="x_codes", align_bytes=64)
+        x_scales = keep.tile([P, S], U8, name="x_scales", align_bytes=64)
+        w_bf = [keep.tile([P, E * P, PACK], BF16, name="w_bf%d" % t, align_bytes=64) for t in range(NT)]
+        w_codes = [keep.tile([P, E * P], U32, name="w_codes%d" % t, align_bytes=64) for t in range(NT)]
+        w_scales = [keep.tile([P, E * P], U8, name="w_scales%d" % t, align_bytes=64) for t in range(NT)]
+        y = [keep.tile([P, S], F32, name="y%d" % t) for t in range(NT)]
+        picked = [[keep.tile([P, T], F32, name="picked%d_%d" % (t, r)) for r in range(3)] for t in range(NT)]
+        pair = [keep.tile([P, T], F32, name="pair%d" % t) for t in range(NT)]
+        warm_in = keep.tile([P, 1], F32, name="warm_in")
+        warm_out = keep.tile([P, 1], F32, name="warm_out")
+
+        nc.gpsimd.memset(warm_in[:], 0.0)
+        nc.scalar.activation(warm_out[:], warm_in[:], GELU)
+
+        x_view = xT.rearrange("(p j) t -> p j t", j=PACK)
+        gate_view = gate.rearrange("(p j) s -> p j s", j=PACK)
+        gate_spans = spans(GATE_CHUNKS)
+
+        def load_gate(i):
+            a, z = gate_spans[i]
+            nc.sync.dma_start(gate_sb[:, a:z], gate_view[:, 0, a:z])
+
+        def load_w(e):
+            nc.sync.dma_start(w_raw[e][:], w[e].rearrange("(p j) n -> p j n", j=PACK))
+
+        nc.sync.dma_start(offs_sb[:], offs)
+        nc.sync.dma_start(x_rows[0][:], x_view[:, 0, :])
+        load_gate(0)
+        for j in range(1, PACK):
+            nc.sync.dma_start(x_rows[j][:], x_view[:, j, :])
+        load_gate(1)
+        load_w(0)
+        nc.sync.dma_start(bias[:, :, 0:E], b.rearrange("(t p) e -> p t e", p=P))
+        load_w(1)
+        load_gate(2)
+        load_w(2)
+        load_w(3)
+        load_gate(3)
+        for e in range(4, E):
+            load_w(e)
+        for r, pos in enumerate((pos1, pos2, pos3)):
+            nc.sync.dma_start(pos_sb[r][:], pos)
+
+        def interleave(dst, src):
+            nc.scalar.copy(
+                dst.rearrange("p (c i) j -> p c j i", i=4),
+                src.rearrange("p j (c i) -> p c j i", i=4),
+            )
+
+        def quantize(codes, scales, src, a, z):
+            nc.vector.quantize_mx(
+                out=codes[:, a:z].bitcast(FP8X4),
+                scales=scales[:, a:z],
+                in_=src[:, a:z, :].rearrange("p c j -> p (c j)"),
+            )
+
+        def round_w(t, e):
+            interleave(w_bf[t][:, e * P : (e + 1) * P, :], w_raw[e][:, :, t * P : (t + 1) * P])
+
+        def quantize_w(t, e0, e1):
+            quantize(w_codes[t], w_scales[t], w_bf[t], e0 * P, e1 * P)
+
+        def expert(t, e, a, z):
+            acc = psum.tile([P, z - a], F32, name="acc")
+            cols = slice(e * P, (e + 1) * P)
+            nc.tensor.matmul_mx(
+                out=acc[:],
+                lhsT=w_codes[t][:, cols].bitcast(FP8X4),
+                lhsT_scale=w_scales[t][:, cols],
+                rhs=x_codes[:, a:z].bitcast(FP8X4),
+                rhs_scale=x_scales[:, a:z],
+                start=True,
+                stop=True,
+            )
+            nc.scalar.activation(y[t][:, a:z], acc[:], GELU, bias=bias[:, t, e : e + 1])
+
+        def gather_slots(a, z):
+            x_gated = ring.tile([P, PACK, z - a], F32, name="x_gated")
+            for j in range(PACK):
+                nc.vector.tensor_tensor(
+                    x_gated[:, j, :],
+                    x_rows[j][:].indirect(offs_sb[:, a // PER_COL : z // PER_COL]),
+                    gate_sb[:, a:z],
+                    MULT,
+                )
+            interleave(x_bf[:, a:z, :], x_gated[:])
+
+        def first_tile(a, z):
+            if a % C == 0:
+                new = range(a // C, (z + C - 1) // C)
+                for e in new:
+                    round_w(0, e)
+                quantize_w(0, new.start, new.stop)
+            quantize(x_codes, x_scales, x_bf, a, z)
+            for s0 in range(a, z, C):
+                expert(0, s0 // C, s0, min(s0 + C, z))
+
+        chunks = spans(SLOT_CHUNKS)
+        gather_slots(*chunks[0])
+        for i in range(1, len(chunks)):
+            gather_slots(*chunks[i])
+            first_tile(*chunks[i - 1])
+        first_tile(*chunks[-1])
+
+        def pick(t, r, a, z):
+            nc.vector.tensor_copy(
+                picked[t][r][:, a:z], y[t][:].indirect(pos_sb[r][:, a // PER_COL : z // PER_COL])
+            )
+
+        def finish(t, a, z, last_engine):
+            nc.gpsimd.tensor_tensor(pair[t][:, a:z], picked[t][0][:, a:z], picked[t][1][:, a:z], ADD)
+            last_engine.tensor_tensor(pair[t][:, a:z], pair[t][:, a:z], picked[t][2][:, a:z], ADD)
+            nc.sync.dma_start(out[t * P : (t + 1) * P, a:z], pair[t][:, a:z])
+
+        for e in range(E):
+            round_w(1, e)
+        for e0 in range(0, E, 2):
+            quantize_w(1, e0, min(e0 + 2, E))
+        for e in reversed(range(E)):
+            round_w(2, e)
+        quantize_w(2, E - 1, E)
+
+        pick(0, 0, 0, T)
+        pick(0, 1, 0, T)
+        quantize_w(2, 0, E - 1)
+        pick(0, 2, 0, T)
+        finish(0, 0, T, nc.gpsimd)
+
+        for e in range(E):
+            expert(1, e, e * C, (e + 1) * C)
+        for r in range(3):
+            pick(1, r, 0, T)
+        finish(1, 0, T, nc.gpsimd)
+
+        for e in range(E):
+            expert(2, e, e * C, (e + 1) * C)
+        for r in range(3):
+            pick(2, r, 0, LAST_SPLIT)
+        finish(2, 0, LAST_SPLIT, nc.gpsimd)
+        for r in range(3):
+            pick(2, r, LAST_SPLIT, T)
+        finish(2, LAST_SPLIT, T, nc.vector)

@@ -22,8 +22,15 @@ MULT = mybir.AluOpType.mult
 ADD = mybir.AluOpType.add
 GELU = mybir.ActivationFunctionType.Gelu_apprx_tanh
 
-SLOT_CHUNKS = [512, 512, 512, 256, 256, 128, 128]
-GATE_CHUNKS = [512, 512, 512, 768]
+SLOT_CHUNKS = [512,512,256,256,256,256,256]
+GATE_CHUNKS = [128,384,512,512,768]
+FIRST_PIECE = 128
+EARLY_TILE1 = [2,1,1,0,2,0,2]
+VECTOR_CHUNKS = 2
+VECTOR_TILE1 = 0
+VECTOR_TILE2 = 1
+TILE2_SPLIT = 5
+LAG = 2
 LAST_SPLIT = 480
 
 
@@ -37,7 +44,7 @@ def tile_moe_pre_lin_gelu_kernel(tc, xT, w, b, gate, offs, pos1, pos2, pos3, out
     with ExitStack() as ctx:
         lists = ctx.enter_context(tc.tile_pool(name="lists", bufs=1))
         keep = ctx.enter_context(tc.tile_pool(name="keep", bufs=1))
-        ring = ctx.enter_context(tc.tile_pool(name="ring", bufs=3))
+        ring = ctx.enter_context(tc.tile_pool(name="ring", bufs=2))
         psum = ctx.enter_context(tc.psum_pool(name="psum", bufs=8))
 
         offs_sb = lists.tile([P, S // PER_COL], U16, name="offs_sb")
@@ -49,11 +56,24 @@ def tile_moe_pre_lin_gelu_kernel(tc, xT, w, b, gate, offs, pos1, pos2, pos3, out
         x_bf = keep.tile([P, S, PACK], BF16, name="x_bf", align_bytes=64)
         x_codes = keep.tile([P, S], U32, name="x_codes", align_bytes=64)
         x_scales = keep.tile([P, S], U8, name="x_scales", align_bytes=64)
-        w_bf = [keep.tile([P, E * P, PACK], BF16, name="w_bf%d" % t, align_bytes=64) for t in range(NT)]
+        early1 = sum(EARLY_TILE1) + VECTOR_TILE1
+        groups = {
+            "tile0": (0, 0, E),
+            "tile1early": (1, 0, early1),
+            "tile1": (1, early1, E),
+            "tile2early": (2, 0, VECTOR_TILE2),
+            "tile2": (2, VECTOR_TILE2, E),
+        }
+        w_bf = {}
+        for key, (t, e0, e1) in groups.items():
+            if e1 > e0:
+                staged = keep.tile([P, (e1 - e0) * P, PACK], BF16, name="w_bf_" + key, tag=key, align_bytes=64)
+                for e in range(e0, e1):
+                    w_bf[t, e] = (staged, e - e0)
         w_codes = [keep.tile([P, E * P], U32, name="w_codes%d" % t, align_bytes=64) for t in range(NT)]
         w_scales = [keep.tile([P, E * P], U8, name="w_scales%d" % t, align_bytes=64) for t in range(NT)]
         y = [keep.tile([P, S], F32, name="y%d" % t) for t in range(NT)]
-        picked = [[keep.tile([P, T], F32, name="picked%d_%d" % (t, r)) for r in range(3)] for t in range(NT)]
+        picked = {}
         pair = [keep.tile([P, T], F32, name="pair%d" % t) for t in range(NT)]
         warm_in = keep.tile([P, 1], F32, name="warm_in")
         warm_out = keep.tile([P, 1], F32, name="warm_out")
@@ -69,123 +89,155 @@ def tile_moe_pre_lin_gelu_kernel(tc, xT, w, b, gate, offs, pos1, pos2, pos3, out
             a, z = gate_spans[i]
             nc.sync.dma_start(gate_sb[:, a:z], gate_view[:, 0, a:z])
 
-        def load_w(e):
-            nc.sync.dma_start(w_raw[e][:], w[e].rearrange("(p j) n -> p j n", j=PACK))
+        def load_x(j):
+            nc.sync.dma_start(x_rows[j][:], x_view[:, j, :])
+
+        def load_w(e, n0, n1):
+            nc.sync.dma_start(w_raw[e][:, :, n0:n1], w[e].rearrange("(p j) n -> p j n", j=PACK)[:, :, n0:n1])
 
         nc.sync.dma_start(offs_sb[:], offs)
-        nc.sync.dma_start(x_rows[0][:], x_view[:, 0, :])
+        load_x(0)
         load_gate(0)
-        for j in range(1, PACK):
-            nc.sync.dma_start(x_rows[j][:], x_view[:, j, :])
         load_gate(1)
-        load_w(0)
+        load_x(3)
+        load_x(2)
         nc.sync.dma_start(bias[:, :, 0:E], b.rearrange("(t p) e -> p t e", p=P))
-        load_w(1)
+        load_w(0, 0, P)
+        load_x(1)
+        load_w(0, P, N)
         load_gate(2)
-        load_w(2)
-        load_w(3)
+        load_w(1, 0, N)
+        load_w(3, 0, N)
         load_gate(3)
-        for e in range(4, E):
-            load_w(e)
+        load_w(2, 0, N)
+        load_w(4, 0, N)
+        load_gate(4)
+        load_w(5, 0, N)
+        load_w(7, 0, N)
+        load_w(8, 0, N)
+        load_w(6, 0, N)
         for r, pos in enumerate((pos1, pos2, pos3)):
             nc.sync.dma_start(pos_sb[r][:], pos)
 
-        def interleave(dst, src):
-            nc.scalar.copy(
+        def interleave(copy, dst, src):
+            copy(
                 dst.rearrange("p (c i) j -> p c j i", i=4),
                 src.rearrange("p j (c i) -> p c j i", i=4),
             )
 
-        def quantize(codes, scales, src, a, z):
-            nc.vector.quantize_mx(
-                out=codes[:, a:z].bitcast(FP8X4),
-                scales=scales[:, a:z],
-                in_=src[:, a:z, :].rearrange("p c j -> p (c j)"),
-            )
+        def quantize(codes, scales, src):
+            nc.vector.quantize_mx(out=codes.bitcast(FP8X4), scales=scales, in_=src.rearrange("p c j -> p (c j)"))
 
-        def round_w(t, e):
-            interleave(w_bf[t][:, e * P : (e + 1) * P, :], w_raw[e][:, :, t * P : (t + 1) * P])
+        def round_w(copy, t, e):
+            staged, at = w_bf[t, e]
+            interleave(copy, staged[:, at * P : (at + 1) * P, :], w_raw[e][:, :, t * P : (t + 1) * P])
 
         def quantize_w(t, e0, e1):
-            quantize(w_codes[t], w_scales[t], w_bf[t], e0 * P, e1 * P)
+            while e0 < e1:
+                n = max(m for m in (1, 2, 4, 8) if m <= e1 - e0)
+                staged, at = w_bf[t, e0]
+                cols = slice(e0 * P, (e0 + n) * P)
+                quantize(w_codes[t][:, cols], w_scales[t][:, cols], staged[:, at * P : (at + n) * P, :])
+                e0 += n
 
-        def expert(t, e, a, z):
-            acc = psum.tile([P, z - a], F32, name="acc")
+        def expert(t, e):
+            acc = psum.tile([P, C], F32, name="acc")
             cols = slice(e * P, (e + 1) * P)
+            slots = slice(e * C, (e + 1) * C)
             nc.tensor.matmul_mx(
                 out=acc[:],
                 lhsT=w_codes[t][:, cols].bitcast(FP8X4),
                 lhsT_scale=w_scales[t][:, cols],
-                rhs=x_codes[:, a:z].bitcast(FP8X4),
-                rhs_scale=x_scales[:, a:z],
+                rhs=x_codes[:, slots].bitcast(FP8X4),
+                rhs_scale=x_scales[:, slots],
                 start=True,
                 stop=True,
             )
-            nc.scalar.activation(y[t][:, a:z], acc[:], GELU, bias=bias[:, t, e : e + 1])
+            nc.scalar.activation(y[t][:, slots], acc[:], GELU, bias=bias[:, t, e : e + 1])
 
-        def gather_slots(a, z):
+        def gather_slots(copy, a, z):
             x_gated = ring.tile([P, PACK, z - a], F32, name="x_gated")
             for j in range(PACK):
-                nc.vector.tensor_tensor(
-                    x_gated[:, j, :],
-                    x_rows[j][:].indirect(offs_sb[:, a // PER_COL : z // PER_COL]),
-                    gate_sb[:, a:z],
-                    MULT,
-                )
-            interleave(x_bf[:, a:z, :], x_gated[:])
+                cuts = [a, FIRST_PIECE, z] if FIRST_PIECE and a == 0 and j == 0 else [a, z]
+                for s0, s1 in zip(cuts, cuts[1:]):
+                    nc.vector.tensor_tensor(
+                        x_gated[:, j, s0 - a : s1 - a],
+                        x_rows[j][:].indirect(offs_sb[:, s0 // PER_COL : s1 // PER_COL]),
+                        gate_sb[:, s0:s1],
+                        MULT,
+                    )
+            interleave(copy, x_bf[:, a:z, :], x_gated[:])
 
         def first_tile(a, z):
-            if a % C == 0:
-                new = range(a // C, (z + C - 1) // C)
-                for e in new:
-                    round_w(0, e)
-                quantize_w(0, new.start, new.stop)
-            quantize(x_codes, x_scales, x_bf, a, z)
-            for s0 in range(a, z, C):
-                expert(0, s0 // C, s0, min(s0 + C, z))
+            quantize_w(0, a // C, z // C)
+            quantize(x_codes[:, a:z], x_scales[:, a:z], x_bf[:, a:z, :])
+            for e in range(a // C, z // C):
+                expert(0, e)
+
+        on_scalar = nc.scalar.copy
+        on_vector = nc.vector.tensor_copy
 
         chunks = spans(SLOT_CHUNKS)
-        gather_slots(*chunks[0])
-        for i in range(1, len(chunks)):
-            gather_slots(*chunks[i])
-            first_tile(*chunks[i - 1])
-        first_tile(*chunks[-1])
+        done1 = 0
+        for i, (a, z) in enumerate(chunks):
+            for e in range(a // C, z // C):
+                round_w(on_scalar, 0, e)
+            gather_slots(on_vector if i >= len(chunks) - VECTOR_CHUNKS else on_scalar, a, z)
+            for e in range(done1, done1 + EARLY_TILE1[i]):
+                round_w(on_scalar, 1, e)
+            done1 += EARLY_TILE1[i]
+            if i >= LAG:
+                first_tile(*chunks[i - LAG])
+        for a, z in chunks[len(chunks) - LAG :]:
+            first_tile(a, z)
+
+        for e in range(done1, early1):
+            round_w(on_vector, 1, e)
+        for e in range(VECTOR_TILE2):
+            round_w(on_vector, 2, e)
+        quantize_w(1, 0, early1)
+        quantize_w(2, 0, VECTOR_TILE2)
+        for e in range(early1, E):
+            round_w(on_scalar, 1, e)
 
         def pick(t, r, a, z):
-            nc.vector.tensor_copy(
-                picked[t][r][:, a:z], y[t][:].indirect(pos_sb[r][:, a // PER_COL : z // PER_COL])
-            )
+            nc.vector.tensor_copy(picked[t][r][:, a:z], y[t][:].indirect(pos_sb[r][:, a // PER_COL : z // PER_COL]))
 
-        def finish(t, a, z, last_engine):
-            nc.gpsimd.tensor_tensor(pair[t][:, a:z], picked[t][0][:, a:z], picked[t][1][:, a:z], ADD)
-            last_engine.tensor_tensor(pair[t][:, a:z], pair[t][:, a:z], picked[t][2][:, a:z], ADD)
+        def fresh(t, r, tag=None):
+            name = "picked%d_%d" % (t, r)
+            return keep.tile([P, T], F32, name=name, tag=tag or name, align_bytes=64)[:]
+
+        def finish(t, a, z, engine):
+            engine.tensor_tensor(pair[t][:, a:z], picked[t][0][:, a:z], picked[t][1][:, a:z], ADD)
+            engine.tensor_tensor(pair[t][:, a:z], pair[t][:, a:z], picked[t][2][:, a:z], ADD)
             nc.sync.dma_start(out[t * P : (t + 1) * P, a:z], pair[t][:, a:z])
 
-        for e in range(E):
-            round_w(1, e)
-        for e0 in range(0, E, 2):
-            quantize_w(1, e0, min(e0 + 2, E))
-        for e in reversed(range(E)):
-            round_w(2, e)
-        quantize_w(2, E - 1, E)
-
+        picked[0] = [fresh(0, 0), fresh(0, 1)]
         pick(0, 0, 0, T)
         pick(0, 1, 0, T)
-        quantize_w(2, 0, E - 1)
+        quantize_w(1, early1, E)
+        for e in range(E):
+            expert(1, e)
+        picked[0].append(fresh(0, 2, "tile1"))
         pick(0, 2, 0, T)
         finish(0, 0, T, nc.gpsimd)
 
-        for e in range(E):
-            expert(1, e, e * C, (e + 1) * C)
-        for r in range(3):
-            pick(1, r, 0, T)
+        picked[1] = [fresh(1, 0)]
+        pick(1, 0, 0, T)
+        for e in range(VECTOR_TILE2, E):
+            round_w(on_scalar, 2, e)
+        quantize_w(2, VECTOR_TILE2, TILE2_SPLIT)
+        quantize_w(2, TILE2_SPLIT, E)
+        both = keep.tile([P, 2, T], F32, name="picked1_late", tag="tile2", align_bytes=64)
+        picked[1].extend([both[:, 0, :], both[:, 1, :]])
+        pick(1, 1, 0, T)
+        pick(1, 2, 0, T)
         finish(1, 0, T, nc.gpsimd)
 
         for e in range(E):
-            expert(2, e, e * C, (e + 1) * C)
-        for r in range(3):
-            pick(2, r, 0, LAST_SPLIT)
-        finish(2, 0, LAST_SPLIT, nc.gpsimd)
-        for r in range(3):
-            pick(2, r, LAST_SPLIT, T)
-        finish(2, LAST_SPLIT, T, nc.vector)
+            expert(2, e)
+        picked[2] = [fresh(2, r) for r in range(3)]
+        for a, z, engine in ((0, LAST_SPLIT, nc.gpsimd), (LAST_SPLIT, T, nc.vector)):
+            for r in range(3):
+                pick(2, r, a, z)
+            finish(2, a, z, engine)

@@ -22,16 +22,17 @@ MULT = mybir.AluOpType.mult
 ADD = mybir.AluOpType.add
 GELU = mybir.ActivationFunctionType.Gelu_apprx_tanh
 
-SLOT_CHUNKS = [512,512,256,256,256,256,256]
+SLOT_CHUNKS = [512,256,256,256,256,256,256,256]
 GATE_CHUNKS = [128,384,512,512,768]
 FIRST_PIECE = 128
-EARLY_TILE1 = [2,1,1,0,2,0,2]
-VECTOR_CHUNKS = 2
+EARLY_TILE1 = [1,0,1,2,2,0,1,2]
+VECTOR_CHUNKS = 0
 VECTOR_TILE1 = 0
-VECTOR_TILE2 = 1
+VECTOR_TILE2 = 0
 TILE2_SPLIT = 5
 LAG = 2
-LAST_SPLIT = 480
+LAST_SPLIT = 384
+LATE_AT = {"tile1": 0, "tile2a": 4, "tile2b": 5}
 
 
 def spans(widths):
@@ -44,7 +45,7 @@ def tile_moe_pre_lin_gelu_kernel(tc, xT, w, b, gate, offs, pos1, pos2, pos3, out
     with ExitStack() as ctx:
         lists = ctx.enter_context(tc.tile_pool(name="lists", bufs=1))
         keep = ctx.enter_context(tc.tile_pool(name="keep", bufs=1))
-        ring = ctx.enter_context(tc.tile_pool(name="ring", bufs=2))
+        ring = ctx.enter_context(tc.tile_pool(name="ring", bufs=3))
         psum = ctx.enter_context(tc.psum_pool(name="psum", bufs=8))
 
         offs_sb = lists.tile([P, S // PER_COL], U16, name="offs_sb")
@@ -62,7 +63,8 @@ def tile_moe_pre_lin_gelu_kernel(tc, xT, w, b, gate, offs, pos1, pos2, pos3, out
             "tile1early": (1, 0, early1),
             "tile1": (1, early1, E),
             "tile2early": (2, 0, VECTOR_TILE2),
-            "tile2": (2, VECTOR_TILE2, E),
+            "tile2a": (2, VECTOR_TILE2, TILE2_SPLIT),
+            "tile2b": (2, TILE2_SPLIT, E),
         }
         w_bf = {}
         for key, (t, e0, e1) in groups.items():
@@ -99,23 +101,23 @@ def tile_moe_pre_lin_gelu_kernel(tc, xT, w, b, gate, offs, pos1, pos2, pos3, out
         load_x(0)
         load_gate(0)
         load_gate(1)
-        load_x(3)
+        load_x(1)
         load_x(2)
         nc.sync.dma_start(bias[:, :, 0:E], b.rearrange("(t p) e -> p t e", p=P))
         load_w(0, 0, P)
-        load_x(1)
-        load_w(0, P, N)
+        load_x(3)
         load_gate(2)
         load_w(1, 0, N)
+        load_w(2, 0, N)
+        load_w(0, P, N)
         load_w(3, 0, N)
         load_gate(3)
-        load_w(2, 0, N)
         load_w(4, 0, N)
         load_gate(4)
         load_w(5, 0, N)
+        load_w(6, 0, N)
         load_w(7, 0, N)
         load_w(8, 0, N)
-        load_w(6, 0, N)
         for r, pos in enumerate((pos1, pos2, pos3)):
             nc.sync.dma_start(pos_sb[r][:], pos)
 
@@ -201,43 +203,53 @@ def tile_moe_pre_lin_gelu_kernel(tc, xT, w, b, gate, offs, pos1, pos2, pos3, out
             round_w(on_scalar, 1, e)
 
         def pick(t, r, a, z):
-            nc.vector.tensor_copy(picked[t][r][:, a:z], y[t][:].indirect(pos_sb[r][:, a // PER_COL : z // PER_COL]))
+            nc.vector.tensor_copy(
+                picked[t, r][:, a:z], y[t][:].indirect(pos_sb[r][:, a // PER_COL : z // PER_COL])
+            )
 
-        def fresh(t, r, tag=None):
-            name = "picked%d_%d" % (t, r)
-            return keep.tile([P, T], F32, name=name, tag=tag or name, align_bytes=64)[:]
+        def new_picked(t, r, tag):
+            picked[t, r] = keep.tile([P, T], F32, name="picked%d_%d" % (t, r), tag=tag, align_bytes=64)
 
-        def finish(t, a, z, engine):
-            engine.tensor_tensor(pair[t][:, a:z], picked[t][0][:, a:z], picked[t][1][:, a:z], ADD)
-            engine.tensor_tensor(pair[t][:, a:z], pair[t][:, a:z], picked[t][2][:, a:z], ADD)
+        def finish(t, a, z, first, second):
+            first.tensor_tensor(pair[t][:, a:z], picked[t, 0][:, a:z], picked[t, 1][:, a:z], ADD)
+            second.tensor_tensor(pair[t][:, a:z], pair[t][:, a:z], picked[t, 2][:, a:z], ADD)
             nc.sync.dma_start(out[t * P : (t + 1) * P, a:z], pair[t][:, a:z])
 
-        picked[0] = [fresh(0, 0), fresh(0, 1)]
-        pick(0, 0, 0, T)
-        pick(0, 1, 0, T)
-        quantize_w(1, early1, E)
-        for e in range(E):
-            expert(1, e)
-        picked[0].append(fresh(0, 2, "tile1"))
-        pick(0, 2, 0, T)
-        finish(0, 0, T, nc.gpsimd)
+        def late_weights(i):
+            freed = []
+            for key, at in LATE_AT.items():
+                t, e0, e1 = groups[key]
+                if at == i:
+                    if t == 2:
+                        for e in range(e0, e1):
+                            round_w(on_scalar, t, e)
+                    quantize_w(t, e0, e1)
+                    if t == 1:
+                        for e in range(E):
+                            expert(1, e)
+                    if e1 > e0:
+                        freed.append(key)
+            return freed
 
-        picked[1] = [fresh(1, 0)]
-        pick(1, 0, 0, T)
-        for e in range(VECTOR_TILE2, E):
-            round_w(on_scalar, 2, e)
-        quantize_w(2, VECTOR_TILE2, TILE2_SPLIT)
-        quantize_w(2, TILE2_SPLIT, E)
-        both = keep.tile([P, 2, T], F32, name="picked1_late", tag="tile2", align_bytes=64)
-        picked[1].extend([both[:, 0, :], both[:, 1, :]])
-        pick(1, 1, 0, T)
-        pick(1, 2, 0, T)
-        finish(1, 0, T, nc.gpsimd)
+        freed = []
+        for i in range(6):
+            t, r = divmod(i, 3)
+            if r == 0:
+                freed = []
+            freed = freed + late_weights(i)
+            tag = freed.pop() if freed and i > 0 else "picked%d" % i
+            new_picked(t, r, tag)
+            pick(t, r, 0, T)
+            if r == 2:
+                finish(t, 0, T, nc.gpsimd, nc.gpsimd)
+        late_weights(6)
 
         for e in range(E):
             expert(2, e)
-        picked[2] = [fresh(2, r) for r in range(3)]
-        for a, z, engine in ((0, LAST_SPLIT, nc.gpsimd), (LAST_SPLIT, T, nc.vector)):
-            for r in range(3):
-                pick(2, r, a, z)
-            finish(2, a, z, engine)
+        for r in range(3):
+            new_picked(2, r, "picked%d" % (6 + r))
+            pick(2, r, 0, LAST_SPLIT)
+        finish(2, 0, LAST_SPLIT, nc.gpsimd, nc.gpsimd)
+        for r in range(3):
+            pick(2, r, LAST_SPLIT, T)
+        finish(2, LAST_SPLIT, T, nc.gpsimd, nc.vector)

from contextlib import ExitStack

import concourse.mybir as mybir

K, T, E, C, N = 512, 768, 9, 256, 384
S = E * C
P = 128
PACK = 4
NT = N // P
PER_COL = 16

FLOPS = 2 * K * N * S
BYTES = 4 * (K * T + E * K * N + N * E + S + N * T) + 2 * P * (S + 3 * T) // PER_COL

F32 = mybir.dt.float32
BF16 = mybir.dt.bfloat16
U32 = mybir.dt.uint32
U16 = mybir.dt.uint16
U8 = mybir.dt.uint8
FP8X4 = mybir.dt.float8_e4m3fn_x4
MULT = mybir.AluOpType.mult
ADD = mybir.AluOpType.add
GELU = mybir.ActivationFunctionType.Gelu_apprx_tanh

SLOT_CHUNKS = [512,256,256,256,256,256,256,256]
GATE_CHUNKS = [128,384,512,512,768]
FIRST_PIECE = 128
EARLY_TILE1 = [1,0,1,2,2,0,1,2]
VECTOR_CHUNKS = 0
VECTOR_TILE1 = 0
VECTOR_TILE2 = 0
TILE2_SPLIT = 5
LAG = 2
LAST_SPLIT = 384
LATE_AT = {"tile1": 0, "tile2a": 4, "tile2b": 5}


def spans(widths):
    starts = [sum(widths[:i]) for i in range(len(widths))]
    return [(a, a + n) for a, n in zip(starts, widths)]


def tile_moe_pre_lin_gelu_kernel(tc, xT, w, b, gate, offs, pos1, pos2, pos3, out):
    nc = tc.nc
    with ExitStack() as ctx:
        lists = ctx.enter_context(tc.tile_pool(name="lists", bufs=1))
        keep = ctx.enter_context(tc.tile_pool(name="keep", bufs=1))
        ring = ctx.enter_context(tc.tile_pool(name="ring", bufs=3))
        psum = ctx.enter_context(tc.psum_pool(name="psum", bufs=8))

        offs_sb = lists.tile([P, S // PER_COL], U16, name="offs_sb")
        pos_sb = [lists.tile([P, T // PER_COL], U16, name="pos_sb%d" % r) for r in range(3)]
        x_rows = [keep.tile([P, T], F32, name="x_rows%d" % j) for j in range(PACK)]
        gate_sb = keep.tile([P, S], F32, name="gate_sb")
        w_raw = [keep.tile([P, PACK, N], F32, name="w_raw%d" % e) for e in range(E)]
        bias = keep.tile([P, NT, 16], F32, name="bias")
        x_bf = keep.tile([P, S, PACK], BF16, name="x_bf", align_bytes=64)
        x_codes = keep.tile([P, S], U32, name="x_codes", align_bytes=64)
        x_scales = keep.tile([P, S], U8, name="x_scales", align_bytes=64)
        early1 = sum(EARLY_TILE1) + VECTOR_TILE1
        groups = {
            "tile0": (0, 0, E),
            "tile1early": (1, 0, early1),
            "tile1": (1, early1, E),
            "tile2early": (2, 0, VECTOR_TILE2),
            "tile2a": (2, VECTOR_TILE2, TILE2_SPLIT),
            "tile2b": (2, TILE2_SPLIT, E),
        }
        w_bf = {}
        for key, (t, e0, e1) in groups.items():
            if e1 > e0:
                staged = keep.tile([P, (e1 - e0) * P, PACK], BF16, name="w_bf_" + key, tag=key, align_bytes=64)
                for e in range(e0, e1):
                    w_bf[t, e] = (staged, e - e0)
        w_codes = [keep.tile([P, E * P], U32, name="w_codes%d" % t, align_bytes=64) for t in range(NT)]
        w_scales = [keep.tile([P, E * P], U8, name="w_scales%d" % t, align_bytes=64) for t in range(NT)]
        y = [keep.tile([P, S], F32, name="y%d" % t) for t in range(NT)]
        picked = {}
        pair = [keep.tile([P, T], F32, name="pair%d" % t) for t in range(NT)]
        warm_in = keep.tile([P, 1], F32, name="warm_in")
        warm_out = keep.tile([P, 1], F32, name="warm_out")

        nc.gpsimd.memset(warm_in[:], 0.0)
        nc.scalar.activation(warm_out[:], warm_in[:], GELU)

        x_view = xT.rearrange("(p j) t -> p j t", j=PACK)
        gate_view = gate.rearrange("(p j) s -> p j s", j=PACK)
        gate_spans = spans(GATE_CHUNKS)

        def load_gate(i):
            a, z = gate_spans[i]
            nc.sync.dma_start(gate_sb[:, a:z], gate_view[:, 0, a:z])

        def load_x(j):
            nc.sync.dma_start(x_rows[j][:], x_view[:, j, :])

        def load_w(e, n0, n1):
            nc.sync.dma_start(w_raw[e][:, :, n0:n1], w[e].rearrange("(p j) n -> p j n", j=PACK)[:, :, n0:n1])

        nc.sync.dma_start(offs_sb[:], offs)
        load_x(0)
        load_gate(0)
        load_gate(1)
        load_x(1)
        load_x(2)
        nc.sync.dma_start(bias[:, :, 0:E], b.rearrange("(t p) e -> p t e", p=P))
        load_w(0, 0, P)
        load_x(3)
        load_gate(2)
        load_w(1, 0, N)
        load_w(2, 0, N)
        load_w(0, P, N)
        load_w(3, 0, N)
        load_gate(3)
        load_w(4, 0, N)
        load_gate(4)
        load_w(5, 0, N)
        load_w(6, 0, N)
        load_w(7, 0, N)
        load_w(8, 0, N)
        for r, pos in enumerate((pos1, pos2, pos3)):
            nc.sync.dma_start(pos_sb[r][:], pos)

        def interleave(copy, dst, src):
            copy(
                dst.rearrange("p (c i) j -> p c j i", i=4),
                src.rearrange("p j (c i) -> p c j i", i=4),
            )

        def quantize(codes, scales, src):
            nc.vector.quantize_mx(out=codes.bitcast(FP8X4), scales=scales, in_=src.rearrange("p c j -> p (c j)"))

        def round_w(copy, t, e):
            staged, at = w_bf[t, e]
            interleave(copy, staged[:, at * P : (at + 1) * P, :], w_raw[e][:, :, t * P : (t + 1) * P])

        def quantize_w(t, e0, e1):
            while e0 < e1:
                n = max(m for m in (1, 2, 4, 8) if m <= e1 - e0)
                staged, at = w_bf[t, e0]
                cols = slice(e0 * P, (e0 + n) * P)
                quantize(w_codes[t][:, cols], w_scales[t][:, cols], staged[:, at * P : (at + n) * P, :])
                e0 += n

        def expert(t, e):
            acc = psum.tile([P, C], F32, name="acc")
            cols = slice(e * P, (e + 1) * P)
            slots = slice(e * C, (e + 1) * C)
            nc.tensor.matmul_mx(
                out=acc[:],
                lhsT=w_codes[t][:, cols].bitcast(FP8X4),
                lhsT_scale=w_scales[t][:, cols],
                rhs=x_codes[:, slots].bitcast(FP8X4),
                rhs_scale=x_scales[:, slots],
                start=True,
                stop=True,
            )
            nc.scalar.activation(y[t][:, slots], acc[:], GELU, bias=bias[:, t, e : e + 1])

        def gather_slots(copy, a, z):
            x_gated = ring.tile([P, PACK, z - a], F32, name="x_gated")
            for j in range(PACK):
                cuts = [a, FIRST_PIECE, z] if FIRST_PIECE and a == 0 and j == 0 else [a, z]
                for s0, s1 in zip(cuts, cuts[1:]):
                    nc.vector.tensor_tensor(
                        x_gated[:, j, s0 - a : s1 - a],
                        x_rows[j][:].indirect(offs_sb[:, s0 // PER_COL : s1 // PER_COL]),
                        gate_sb[:, s0:s1],
                        MULT,
                    )
            interleave(copy, x_bf[:, a:z, :], x_gated[:])

        def first_tile(a, z):
            quantize_w(0, a // C, z // C)
            quantize(x_codes[:, a:z], x_scales[:, a:z], x_bf[:, a:z, :])
            for e in range(a // C, z // C):
                expert(0, e)

        on_scalar = nc.scalar.copy
        on_vector = nc.vector.tensor_copy

        chunks = spans(SLOT_CHUNKS)
        done1 = 0
        for i, (a, z) in enumerate(chunks):
            for e in range(a // C, z // C):
                round_w(on_scalar, 0, e)
            gather_slots(on_vector if i >= len(chunks) - VECTOR_CHUNKS else on_scalar, a, z)
            for e in range(done1, done1 + EARLY_TILE1[i]):
                round_w(on_scalar, 1, e)
            done1 += EARLY_TILE1[i]
            if i >= LAG:
                first_tile(*chunks[i - LAG])
        for a, z in chunks[len(chunks) - LAG :]:
            first_tile(a, z)

        for e in range(done1, early1):
            round_w(on_vector, 1, e)
        for e in range(VECTOR_TILE2):
            round_w(on_vector, 2, e)
        quantize_w(1, 0, early1)
        quantize_w(2, 0, VECTOR_TILE2)
        for e in range(early1, E):
            round_w(on_scalar, 1, e)

        def pick(t, r, a, z):
            nc.vector.tensor_copy(
                picked[t, r][:, a:z], y[t][:].indirect(pos_sb[r][:, a // PER_COL : z // PER_COL])
            )

        def new_picked(t, r, tag):
            picked[t, r] = keep.tile([P, T], F32, name="picked%d_%d" % (t, r), tag=tag, align_bytes=64)

        def finish(t, a, z, first, second):
            first.tensor_tensor(pair[t][:, a:z], picked[t, 0][:, a:z], picked[t, 1][:, a:z], ADD)
            second.tensor_tensor(pair[t][:, a:z], pair[t][:, a:z], picked[t, 2][:, a:z], ADD)
            nc.sync.dma_start(out[t * P : (t + 1) * P, a:z], pair[t][:, a:z])

        def late_weights(i):
            freed = []
            for key, at in LATE_AT.items():
                t, e0, e1 = groups[key]
                if at == i:
                    if t == 2:
                        for e in range(e0, e1):
                            round_w(on_scalar, t, e)
                    quantize_w(t, e0, e1)
                    if t == 1:
                        for e in range(E):
                            expert(1, e)
                    if e1 > e0:
                        freed.append(key)
            return freed

        freed = []
        for i in range(6):
            t, r = divmod(i, 3)
            if r == 0:
                freed = []
            freed = freed + late_weights(i)
            tag = freed.pop() if freed and i > 0 else "picked%d" % i
            new_picked(t, r, tag)
            pick(t, r, 0, T)
            if r == 2:
                finish(t, 0, T, nc.gpsimd, nc.gpsimd)
        late_weights(6)

        for e in range(E):
            expert(2, e)
        for r in range(3):
            new_picked(2, r, "picked%d" % (6 + r))
            pick(2, r, 0, LAST_SPLIT)
        finish(2, 0, LAST_SPLIT, nc.gpsimd, nc.gpsimd)
        for r in range(3):
            pick(2, r, LAST_SPLIT, T)
        finish(2, LAST_SPLIT, T, nc.gpsimd, nc.vector)
